import numpy as np, ml_dtypes
CORES = [6,7,14,15,22,23,30,31,38,39,46,47,54,55,62,63]
N = 16
ROOT = 15
def setup_inputs(rng):
    return {"x": rng.standard_normal((N, 128, N * 8), dtype=np.float32).astype(ml_dtypes.bfloat16)}
def reference(x):
    return {"y": np.stack([x[ROOT][:, r * 8:(r + 1) * 8] for r in range(N)])}

@@ -1,0 +1,52 @@
+from concourse.bass import DstId, RemoteDMATransfer
+
+P = 4
+W = 128 // P
+RPG = 16 // P
+ENG = 8 // P
+
+SCRATCH = {
+    "stage": ("dram", [P, 128, W], "bfloat16"),
+    "land": ("dram", [128, W], "bfloat16"),
+}
+SEMAPHORES = ["loaded", "sent", "arrived", "stored"]
+
+
+def rank_program(g, core, T, topo):
+    rank = T.rank_of(core)
+    if rank is None:
+        return
+    root_rank = 15
+    root = T.cores[root_rank]
+
+    if core != root:
+        q = rank % RPG
+        g.sync.wait_ge(T.sem.arrived, ENG)
+        g.sync.dma_start(T.y[:], T.land[:, 8 * q:8 * q + 8]).then_inc(T.sem.stored, 16)
+        g.sync.wait_ge(T.sem.stored, 16)
+        return
+
+    queues = [g.sync, g.scalar]
+    for j in range(P):
+        queues[j % 2].dma_start(T.stage[j], T.x[:, j * W:(j + 1) * W]).then_inc(T.sem.loaded, 16)
+    g.wait_ge(T.sem.loaded, 16 * P)
+
+    transfers = []
+    for j in range(P):
+        dsts = [T.cores[r] for r in range(j * RPG, (j + 1) * RPG) if r != root_rank]
+        ids = []
+        for d in dsts:
+            rid, pid, _se = topo.addr(d)
+            ids.append(DstId(rid=rid, pnc=pid))
+        transfers.append(RemoteDMATransfer(
+            dst_ids=ids,
+            dma_engine_mask=((1 << ENG) - 1) << (j * ENG),
+            remote_sem=T.sem.arrived,
+            srcs=[T.stage[j]],
+            dsts=[T.land[:] for _d in dsts],
+        ))
+    g.remote_dma_fused(transfers, local_sem=T.sem.sent)
+
+    g.sync.wait_ge(T.sem.sent, 8)
+    g.sync.dma_start(T.y[:], T.x[:, 8 * root_rank:8 * root_rank + 8]).then_inc(T.sem.stored, 16)
+    g.sync.wait_ge(T.sem.stored, 16)

@@ -3,13 +3,14 @@ from concourse.bass import DstId, RemoteDMATransfer
 P = 4
 W = 128 // P
 RPG = 16 // P
-ENG = 8 // P
+WAVES = [[0, 1], [2, 3]]
+ENG = 4
 
 SCRATCH = {
     "stage": ("dram", [P, 128, W], "bfloat16"),
     "land": ("dram", [128, W], "bfloat16"),
 }
-SEMAPHORES = ["loaded", "sent", "arrived", "stored"]
+SEMAPHORES = ["loaded0", "loaded1", "sent", "arrived", "stored"]
 
 
 def rank_program(g, core, T, topo):
@@ -27,26 +28,28 @@ def rank_program(g, core, T, topo):
         return
 
     queues = [g.sync, g.scalar]
-    for j in range(P):
-        queues[j % 2].dma_start(T.stage[j], T.x[:, j * W:(j + 1) * W]).then_inc(T.sem.loaded, 16)
-    g.wait_ge(T.sem.loaded, 16 * P)
+    for w, groups in enumerate(WAVES):
+        for k, j in enumerate(groups):
+            queues[k].dma_start(T.stage[j], T.x[:, j * W:(j + 1) * W]).then_inc(T.sem["loaded%d" % w], 16)
 
-    transfers = []
-    for j in range(P):
-        dsts = [T.cores[r] for r in range(j * RPG, (j + 1) * RPG) if r != root_rank]
-        ids = []
-        for d in dsts:
-            rid, pid, _se = topo.addr(d)
-            ids.append(DstId(rid=rid, pnc=pid))
-        transfers.append(RemoteDMATransfer(
-            dst_ids=ids,
-            dma_engine_mask=((1 << ENG) - 1) << (j * ENG),
-            remote_sem=T.sem.arrived,
-            srcs=[T.stage[j]],
-            dsts=[T.land[:] for _d in dsts],
-        ))
-    g.remote_dma_fused(transfers, local_sem=T.sem.sent)
+    for w, groups in enumerate(WAVES):
+        g.wait_ge(T.sem["loaded%d" % w], 16 * len(groups))
+        transfers = []
+        for k, j in enumerate(groups):
+            dsts = [T.cores[r] for r in range(j * RPG, (j + 1) * RPG) if r != root_rank]
+            ids = []
+            for d in dsts:
+                rid, pid, _se = topo.addr(d)
+                ids.append(DstId(rid=rid, pnc=pid))
+            transfers.append(RemoteDMATransfer(
+                dst_ids=ids,
+                dma_engine_mask=((1 << ENG) - 1) << (k * ENG),
+                remote_sem=T.sem.arrived,
+                srcs=[T.stage[j]],
+                dsts=[T.land[:] for _d in dsts],
+            ))
+        g.remote_dma_fused(transfers, local_sem=T.sem.sent)
 
-    g.sync.wait_ge(T.sem.sent, 8)
+    g.sync.wait_ge(T.sem.sent, 8 * len(WAVES))
     g.sync.dma_start(T.y[:], T.x[:, 8 * root_rank:8 * root_rank + 8]).then_inc(T.sem.stored, 16)
     g.sync.wait_ge(T.sem.stored, 16)

from concourse.bass import DstId, RemoteDMATransfer

P = 4
W = 128 // P
RPG = 16 // P
WAVES = [[0, 1], [2, 3]]
ENG = 4

SCRATCH = {
    "stage": ("dram", [P, 128, W], "bfloat16"),
    "land": ("dram", [128, W], "bfloat16"),
}
SEMAPHORES = ["loaded0", "loaded1", "sent", "arrived", "stored"]


def rank_program(g, core, T, topo):
    rank = T.rank_of(core)
    if rank is None:
        return
    root_rank = 15
    root = T.cores[root_rank]

    if core != root:
        q = rank % RPG
        g.sync.wait_ge(T.sem.arrived, ENG)
        g.sync.dma_start(T.y[:], T.land[:, 8 * q:8 * q + 8]).then_inc(T.sem.stored, 16)
        g.sync.wait_ge(T.sem.stored, 16)
        return

    queues = [g.sync, g.scalar]
    for w, groups in enumerate(WAVES):
        for k, j in enumerate(groups):
            queues[k].dma_start(T.stage[j], T.x[:, j * W:(j + 1) * W]).then_inc(T.sem["loaded%d" % w], 16)

    for w, groups in enumerate(WAVES):
        g.wait_ge(T.sem["loaded%d" % w], 16 * len(groups))
        transfers = []
        for k, j in enumerate(groups):
            dsts = [T.cores[r] for r in range(j * RPG, (j + 1) * RPG) if r != root_rank]
            ids = []
            for d in dsts:
                rid, pid, _se = topo.addr(d)
                ids.append(DstId(rid=rid, pnc=pid))
            transfers.append(RemoteDMATransfer(
                dst_ids=ids,
                dma_engine_mask=((1 << ENG) - 1) << (k * ENG),
                remote_sem=T.sem.arrived,
                srcs=[T.stage[j]],
                dsts=[T.land[:] for _d in dsts],
            ))
        g.remote_dma_fused(transfers, local_sem=T.sem.sent)

    g.sync.wait_ge(T.sem.sent, 8 * len(WAVES))
    g.sync.dma_start(T.y[:], T.x[:, 8 * root_rank:8 * root_rank + 8]).then_inc(T.sem.stored, 16)
    g.sync.wait_ge(T.sem.stored, 16)
